import numpy as np
import ml_dtypes


def mxq(x, axis, fmt="e4m3"):
    dtype, down = {"e4m3": (ml_dtypes.float8_e4m3fn, 7), "e5m2": (ml_dtypes.float8_e5m2, 14)}[fmt]
    v = np.moveaxis(np.asarray(x, np.float32).astype(ml_dtypes.bfloat16).astype(np.float64), axis, -1)
    blocks = v.reshape(v.shape[:-1] + (-1, 32))
    amax = np.abs(blocks).max(-1, keepdims=True)
    byte = np.maximum(np.where(amax > 0, np.frexp(amax)[1] - 1 + 127, 0) - down, 1)
    scale = np.exp2(byte - 127.0)
    codes = (blocks / scale).astype(np.float32).astype(dtype).astype(np.float64)
    return np.moveaxis((codes * scale).reshape(v.shape), -1, axis)


WIDE = False


def mx_kscale(k):
    if not WIDE:
        return np.ones(k)
    levels = np.array([10, -10, 5, -5, 0])
    if k % 512:
        return np.exp2(np.random.permutation(np.resize(levels, k // 32))).repeat(32)
    a = np.empty((k // 512, 16))
    for p in range(k // 512):
        a[p, :8] = np.random.permutation(np.resize(levels, 8))
        for g in range(8):
            far = levels[np.abs(levels - a[p, g]) >= 10]
            a[p, g + 8] = far[np.random.randint(len(far))]
    return np.exp2(a.ravel()).repeat(32)


def f64(x):
    return np.asarray(x).astype(np.float64)


def striped(idx):
    return np.tile(np.asarray(idx).reshape(-1, 16).T, (8, 1)).astype(np.uint16)


def unstriped(offs):
    return offs[:16].T.reshape(-1).astype(np.int64)


def striped8(idx):
    return np.asarray(idx).reshape(8, -1, 16).transpose(0, 2, 1).reshape(128, -1).astype(np.uint16)


def unstriped8(offs):
    return offs.reshape(8, 16, -1).transpose(0, 2, 1).reshape(8, -1).astype(np.int64)


def pick8(x, idx, run):
    r = np.arange(len(x))
    return x[r[:, None], idx[r % (8 * run) // run]]


E2M1 = np.array([0.0, 0.5, 1.0, 1.5, 2.0, 3.0, 4.0, 6.0, -0.0, -0.5, -1.0, -1.5, -2.0, -3.0, -4.0, -6.0])


def pack_weight(w, fmt):
    k, n = w.shape
    w = f64(np.asarray(w, np.float32).astype(ml_dtypes.bfloat16)).reshape(k // 32, 32, n)
    amax = np.abs(w).max(1)
    if fmt == "e4m3":
        byte = np.frexp(amax)[1] - 1 + 127 - 7
    else:
        mant, ex = np.frexp(amax / 6.0)
        byte = np.where(mant > 0.5, ex, ex - 1) + 127
    byte = np.clip(np.where(amax > 0, byte, 1), 1, 254)
    scaled = (w * np.exp2(127.0 - byte)[:, None, :]).reshape(k, n).astype(np.float32)
    by_word = np.ascontiguousarray(scaled.reshape(k // 512, 128, 4, n).transpose(0, 1, 3, 2))
    if fmt == "e4m3":
        words = by_word.astype(ml_dtypes.float8_e4m3fn).view(np.uint8)
    else:
        c = by_word.astype(ml_dtypes.float4_e2m1fn).view(np.uint8) & 0xF
        words = (c[..., 0::2] | (c[..., 1::2] << 4)).reshape(k // 512, 128, 2 * n)
    return np.ascontiguousarray(words), np.ascontiguousarray(byte.astype(np.uint8).reshape(k // 512, 16, n))


def unpack_weight(words, scales, fmt):
    g, _, n = scales.shape
    words = np.ascontiguousarray(words).reshape(g, 128, n, -1)
    if fmt == "e4m3":
        vals = words.view(ml_dtypes.float8_e4m3fn).astype(np.float64)
    else:
        nib = np.empty((g, 128, n, 4), np.uint8)
        nib[..., 0::2] = words & 0xF
        nib[..., 1::2] = words >> 4
        vals = E2M1[nib]
    vals = vals * np.repeat(np.exp2(scales.astype(np.float64) - 127.0), 8, axis=1)[..., None]
    return vals.transpose(0, 1, 3, 2).reshape(g * 512, n)


def sgn(shape):
    return np.random.uniform(0.5, 2.0, shape) * np.where(np.random.standard_normal(shape) < 0, -1.0, 1.0)


K, J, R, T, U, O, N, S = 512, 512, 512, 1024, 1024, 256, 256, 1024


def setup_inputs():
    n = np.random.standard_normal
    idx = np.stack([np.random.permutation(T)[:J] for _ in range(8)])
    idx2 = np.stack([np.random.permutation(U)[:J] for _ in range(8)])
    idx3 = np.stack([np.random.permutation(U)[:J] for _ in range(8)])
    idx4 = np.stack([np.random.permutation(J)[:O] for _ in range(8)])
    idx5 = np.stack([np.random.permutation(J)[:O] for _ in range(8)])
    idx6 = np.stack([np.random.permutation(J)[:O] for _ in range(8)])
    idx7 = np.random.permutation(S)[:N]
    fk = mx_kscale(K)
    fr = mx_kscale(R)
    wp = pack_weight(n((K, R)) * 1 / np.sqrt(K) / fk[:, None] * fr, "e2m1")
    vsp = pack_weight(n((R, S)) * 1 / np.sqrt(R) / fr[:, None], "e4m3")
    return {
        "ta": (np.random.randint(-7, 8, (K, T)).astype(np.float64)).astype(np.float32),
        "ga": ((np.random.randint(8, 25, (K, 1)) / 64.0) * fk[:, None]).astype(np.float32),
        "gb": (np.random.uniform(0.5, 1.6, (K, 1))).astype(np.float32),
        "w_words": wp[0],
        "w_scales": wp[1],
        "sa": (sgn((R, 1))).astype(np.float32),
        "sb": (sgn((R, 1))).astype(np.float32),
        "sd": (sgn((R, 1))).astype(np.float32),
        "vs_words": vsp[0],
        "vs_scales": vsp[1],
        "offs": striped8(idx),
        "offs2": striped8(idx2),
        "offs3": striped8(idx3),
        "offs4": striped8(idx4),
        "offs5": striped8(idx5),
        "offs6": striped8(idx6),
        "offs7": striped(idx7),
    }


def reference(ta, ga, gb, w_words, w_scales, sa, sb, sd, vs_words, vs_scales, offs, offs2, offs3, offs4, offs5, offs6, offs7):
    idx = unstriped8(offs)
    idx2 = unstriped8(offs2)
    idx3 = unstriped8(offs3)
    idx4 = unstriped8(offs4)
    idx5 = unstriped8(offs5)
    idx6 = unstriped8(offs6)
    idx7 = unstriped(offs7)
    wu = unpack_weight(w_words, w_scales, "e2m1")
    vsu = unpack_weight(vs_words, vs_scales, "e4m3")
    xcd = pick8(f64(ta), idx, 64) * f64(ga)
    xcp = np.zeros((K, U))
    xcp[np.arange(K)[:, None], idx2[np.arange(K) % 512 // 64]] = xcd
    xc = pick8(xcp, idx3, 64) * f64(gb)
    xcq = mxq(xc, 0, "e4m3")
    a = wu.T @ xcq
    hid = np.maximum(pick8(a, idx4, 64) * f64(sa) + pick8(a, idx5, 64) * f64(sb) + pick8(a, idx6, 64) * f64(sd), 0.0)
    vsidx7g = vsu[:, idx7]
    hidq = mxq(hid, 0, "e4m3")
    y = vsidx7g.T @ hidq
    return y

@@ -1,0 +1,216 @@
+from contextlib import ExitStack
+
+import concourse.mybir as mybir
+
+K, J, R, T, U, O, N, S = 512, 512, 512, 1024, 1024, 256, 256, 1024
+FLOPS = 2 * K * R * J + 2 * R * N * O
+
+F32 = mybir.dt.float32
+BF16 = mybir.dt.bfloat16
+I32 = mybir.dt.int32
+U32 = mybir.dt.uint32
+U16 = mybir.dt.uint16
+U8 = mybir.dt.uint8
+FP8X4 = mybir.dt.float8_e4m3fn_x4
+FP4X4 = mybir.dt.float4_e2m1fn_x4
+COPY = mybir.ActivationFunctionType.Copy
+ADD = mybir.AluOpType.add
+
+P = 128
+PACK = 4
+LANES = 16
+JH = J // 2
+OH = O // 2
+PAGES = 3
+
+
+def tile_picked_codepage_plain_one_grouptriple_store_plain_kernel(
+    tc, ta, ga, gb, w_words, w_scales, sa, sb, sd, vs_words, vs_scales,
+    offs, offs2, offs3, offs4, offs5, offs6, offs7, out,
+):
+    nc = tc.nc
+    with ExitStack() as ctx:
+        lists = ctx.enter_context(tc.tile_pool(name="lists", bufs=1))
+        sbuf = ctx.enter_context(tc.tile_pool(name="sbuf", bufs=1))
+        psum = ctx.enter_context(tc.psum_pool(name="psum", bufs=1))
+
+        def load_list(src, name):
+            tile = lists.tile(list(src.shape), U16, name=name)
+            nc.sync.dma_start(tile[:], src)
+            return tile
+
+        def load_factor(queue, src, name):
+            tile = sbuf.tile([P, PACK], F32, name=name)
+            queue.dma_start(tile[:], src.rearrange("(p t) o -> p (t o)", t=PACK))
+            return tile
+
+        def load_scale_rows(tile, src):
+            for q in range(4):
+                nc.sync.dma_start(tile[32 * q : 32 * q + 4, :].bitcast(I32), src[0, 4 * q : 4 * q + 4, :].bitcast(I32))
+
+        ta_rows = ta.rearrange("(p t) c -> p t c", t=PACK)
+
+        def load_table(queue, t):
+            tile = sbuf.tile([P, T], F32, name=f"table{t}")
+            queue.dma_start(tile[:], ta_rows[:, t, :])
+            return tile
+
+        page = [sbuf.tile([P, U], F32, name=f"page{t}") for t in range(PAGES)]
+        page.append(page[0])
+        w_scale_raw = sbuf.tile([P, R], U8, name="w_scale_raw", align_bytes=64)
+        vs_scale_raw = sbuf.tile([P, S], U8, name="vs_scale_raw", align_bytes=64)
+        nc.vector.memset(page[0][:], 0.0)
+        nc.vector.memset(w_scale_raw[:].bitcast(I32), 0)
+        nc.vector.memset(vs_scale_raw[:].bitcast(I32), 0)
+        for t in range(1, PAGES):
+            nc.vector.memset(page[t][:], 0.0)
+
+        table = [load_table(nc.scalar, 0)]
+        l1 = load_list(offs, "l1")
+        ga_t = load_factor(nc.sync, ga, "ga_t")
+        l2 = load_list(offs2, "l2")
+        table.append(load_table(nc.scalar, 1))
+        l3 = load_list(offs3, "l3")
+        gb_t = load_factor(nc.sync, gb, "gb_t")
+        l7 = load_list(offs7, "l7")
+        table.append(load_table(nc.sync, 2))
+        table.append(load_table(nc.sync, 3))
+        w_raw = sbuf.tile([P, 2 * R], U8, name="w_raw", align_bytes=64)
+        nc.sync.dma_start(w_raw[:].bitcast(I32), w_words[0].bitcast(I32))
+        load_scale_rows(w_scale_raw, w_scales)
+        vs_raw = sbuf.tile([P, S], I32, name="vs_raw", align_bytes=64)
+        nc.sync.dma_start(vs_raw[:], vs_words[0].rearrange("p n t -> p (n t)").bitcast(I32))
+        l4 = load_list(offs4, "l4")
+        l5 = load_list(offs5, "l5")
+        l6 = load_list(offs6, "l6")
+        sa_t = load_factor(nc.sync, sa, "sa_t")
+        sb_t = load_factor(nc.sync, sb, "sb_t")
+        sd_t = load_factor(nc.sync, sd, "sd_t")
+        load_scale_rows(vs_scale_raw, vs_scales)
+
+        def fetch(dst, window, offsets, first, count, factor, t):
+            cols = slice(first // LANES, (first + count) // LANES)
+            nc.scalar.activation(dst, window[:].indirect(offsets[:, cols]), COPY, scale=factor[:, t : t + 1])
+
+        xcd = [sbuf.tile([P, J], F32, name=f"xcd{t}", align_bytes=64) for t in range(PACK)]
+        for h in range(2):
+            js = slice(h * JH, (h + 1) * JH)
+            fetch(xcd[0][:, js], table[0], l1, h * JH, JH, ga_t, 0)
+            nc.vector.tensor_copy(page[0][:].indirect(l2[:, h * JH // LANES : (h + 1) * JH // LANES]), xcd[0][:, js])
+        for t in range(1, PACK):
+            fetch(xcd[t][:], table[t], l1, 0, J, ga_t, t)
+        for t in range(1, PAGES):
+            nc.vector.tensor_copy(page[t][:].indirect(l2[:]), xcd[t][:])
+
+        xc01 = sbuf.tile([P, 2, J], BF16, name="xc01", tag="table3")
+        xc_woven = sbuf.tile([P, J, PACK], BF16, name="xc_woven", align_bytes=64)
+        for t in range(2):
+            fetch(xc01[:, t, :], page[t], l3, 0, J, gb_t, t)
+        nc.vector.tensor_copy(page[3][:].indirect(l2[:]), xcd[3][:])
+        nc.scalar.copy(xc_woven[:, :, 0:2], xc01[:].rearrange("p t j -> p j t"))
+        w_dealt = sbuf.tile([P, 2 * R], U8, name="w_dealt", align_bytes=64)
+        nc.scalar.copy(
+            w_dealt[:].bitcast(U16).rearrange("p (t m) -> p t m", t=PACK),
+            w_raw[:].bitcast(U16).rearrange("p (m t) -> p t m", t=PACK),
+        )
+        xc23 = sbuf.tile([P, 2, J], BF16, name="xc23", tag="table3")
+        fetch(xc23[:, 0, :], page[2], l3, 0, J, gb_t, 2)
+        w_scale = sbuf.tile([P, R], U8, name="w_scale", tag="xcd3", align_bytes=64)
+        nc.vector.tensor_copy(
+            w_scale[:].rearrange("p (t m) -> p t m", t=PACK),
+            w_scale_raw[:].rearrange("p (m t) -> p t m", t=PACK),
+        )
+        xc_codes = sbuf.tile([P, J], U32, name="xc_codes", align_bytes=64)
+        xc_scale = sbuf.tile([P, J], U8, name="xc_scale", align_bytes=64)
+        for h in range(2):
+            js = slice(h * JH, (h + 1) * JH)
+            fetch(xc23[:, 1, js], page[3], l3, h * JH, JH, gb_t, 3)
+            nc.vector.tensor_copy(xc_woven[:, js, 2:4], xc23[:, :, js].rearrange("p t j -> p j t"))
+        pieces = [slice(0, JH), slice(JH, JH + JH // 2), slice(JH + JH // 2, J)]
+        for js in pieces:
+            nc.vector.quantize_mx(
+                out=xc_codes[:, js].bitcast(FP8X4), scales=xc_scale[:, js],
+                in_=xc_woven[:, js, :].rearrange("p j t -> p (j t)"),
+            )
+
+        def first_product(dst, t, js):
+            nc.tensor.matmul_mx(
+                out=dst,
+                lhsT=w_dealt[:, 2 * P * t : 2 * P * (t + 1)].bitcast(FP4X4),
+                lhsT_scale=w_scale[:, P * t : P * (t + 1)],
+                rhs=xc_codes[:, js].bitcast(FP8X4), rhs_scale=xc_scale[:, js],
+                start=True, stop=True,
+            )
+
+        a = [sbuf.tile([P, J], F32, name=f"a{t}") for t in range(PACK)]
+        for h, js in enumerate(pieces):
+            bank = psum.tile([P, js.stop - js.start], F32, name=f"a0_bank{h}")
+            first_product(bank[:], 0, js)
+            nc.scalar.activation(a[0][:, js], bank[:], COPY)
+
+        vs_codes = sbuf.tile([P, N], U32, name="vs_codes", tag="xc_woven", align_bytes=64)
+        nc.vector.tensor_copy(vs_codes[:], vs_raw[:].bitcast(U32).indirect(l7[:]))
+        for t in range(1, PACK):
+            bank = psum.tile([P, J], F32, name=f"a_bank{t}")
+            first_product(bank[:], t, slice(0, J))
+            nc.vector.tensor_copy(a[t][:], bank[:])
+
+        hid_woven = sbuf.tile([P, O, PACK], BF16, name="hid_woven", align_bytes=64)
+
+        def triple_sum(dst, t, first, count, name):
+            parts = [sbuf.tile([P, count], F32, name=f"{name}_part{i}", align_bytes=64) for i in range(3)]
+            two = sbuf.tile([P, count], F32, name=f"{name}_two")
+            fetch(parts[0][:], a[t], l4, first, count, sa_t, t)
+            fetch(parts[1][:], a[t], l5, first, count, sb_t, t)
+            nc.vector.tensor_tensor(two[:], parts[0][:], parts[1][:], ADD)
+            fetch(parts[2][:], a[t], l6, first, count, sd_t, t)
+            nc.vector.tensor_tensor(dst, two[:], parts[2][:], ADD)
+
+        sum01 = sbuf.tile([P, 2, O], F32, name="sum01")
+        triple_sum(sum01[:, 0, :], 0, 0, O, "s0")
+        vs_scale = sbuf.tile([P, N], U8, name="vs_scale", tag="s0_part0", align_bytes=64)
+        nc.vector.tensor_copy(vs_scale[:], vs_scale_raw[:].indirect(l7[:]))
+        triple_sum(sum01[:, 1, :], 1, 0, O, "s1")
+        nc.vector.tensor_scalar_max(hid_woven[:, :, 0:2], sum01[:].rearrange("p t o -> p o t"), 0.0)
+
+        hid_codes = sbuf.tile([P, O], U32, name="hid_codes", align_bytes=64)
+        hid_scale = sbuf.tile([P, O], U8, name="hid_scale", align_bytes=64)
+        out_rows = out.rearrange("(m p) o -> p m o", p=P)
+
+        def second_product(dst, m, os_):
+            nc.tensor.matmul_mx(
+                out=dst,
+                lhsT=vs_codes[:, P * m : P * (m + 1)].bitcast(FP8X4),
+                lhsT_scale=vs_scale[:, P * m : P * (m + 1)],
+                rhs=hid_codes[:, os_].bitcast(FP8X4), rhs_scale=hid_scale[:, os_],
+                start=True, stop=True,
+            )
+
+        for h in range(2):
+            os_ = slice(h * OH, (h + 1) * OH)
+            sum23 = sbuf.tile([P, 2, OH], F32, name=f"sum23_{h}")
+            for t in range(2, PACK):
+                triple_sum(sum23[:, t - 2, :], t, h * OH, OH, f"s{t}{h}")
+            nc.vector.tensor_scalar_max(hid_woven[:, os_, 2:4], sum23[:].rearrange("p t o -> p o t"), 0.0)
+            nc.vector.quantize_mx(
+                out=hid_codes[:, os_].bitcast(FP8X4), scales=hid_scale[:, os_],
+                in_=hid_woven[:, os_, :].rearrange("p o t -> p (o t)"),
+            )
+            if h == 0:
+                bank0 = psum.tile([P, 2, OH], F32, name="y_bank", tag="a0_bank0")
+                for m in range(2):
+                    second_product(bank0[:, m, :], m, os_)
+            else:
+                y0 = sbuf.tile([P, 2, OH], F32, name="y0")
+                nc.scalar.activation(y0[:], bank0[:], COPY)
+                nc.sync.dma_start(out_rows[:, :, 0:OH], y0[:])
+                for m in range(2):
+                    bank = psum.tile([P, OH], F32, name=f"y1_bank{m}")
+                    y = sbuf.tile([P, OH], F32, name=f"y1{m}")
+                    second_product(bank[:], m, os_)
+                    if m == 0:
+                        nc.vector.tensor_copy(y[:], bank[:])
+                        nc.sync.dma_start(out_rows[:, m, os_], y[:])
+                    else:
+                        nc.scalar.activation(y[:], bank[:], COPY)
+                        nc.scalar.dma_start(out_rows[:, m, os_], y[:])

@@ -59,6 +59,8 @@ def tile_picked_codepage_plain_one_grouptriple_store_plain_kernel(
         page.append(page[0])
         w_scale_raw = sbuf.tile([P, R], U8, name="w_scale_raw", align_bytes=64)
         vs_scale_raw = sbuf.tile([P, S], U8, name="vs_scale_raw", align_bytes=64)
+        warm = sbuf.tile([P, 2], F32, name="warm")
+        nc.vector.memset(warm[:, 0:1], 0.0)
         nc.vector.memset(page[0][:], 0.0)
         nc.vector.memset(w_scale_raw[:].bitcast(I32), 0)
         nc.vector.memset(vs_scale_raw[:].bitcast(I32), 0)
@@ -70,6 +72,7 @@ def tile_picked_codepage_plain_one_grouptriple_store_plain_kernel(
         ga_t = load_factor(nc.sync, ga, "ga_t")
         l2 = load_list(offs2, "l2")
         table.append(load_table(nc.scalar, 1))
+        nc.scalar.activation(warm[:, 1:2], warm[:, 0:1], COPY)
         l3 = load_list(offs3, "l3")
         gb_t = load_factor(nc.sync, gb, "gb_t")
         l7 = load_list(offs7, "l7")

@@ -128,8 +128,9 @@ def tile_picked_codepage_plain_one_grouptriple_store_plain_kernel(
         for h in range(2):
             js = slice(h * JH, (h + 1) * JH)
             fetch(xc23[:, 1, js], page[3], l3, h * JH, JH, gb_t, 3)
-            nc.vector.tensor_copy(xc_woven[:, js, 2:4], xc23[:, :, js].rearrange("p t j -> p j t"))
         pieces = [slice(0, JH), slice(JH, JH + JH // 2), slice(JH + JH // 2, J)]
+        for js, weave in zip(pieces, (nc.vector.tensor_copy, nc.vector.tensor_copy, nc.scalar.copy)):
+            weave(xc_woven[:, js, 2:4], xc23[:, :, js].rearrange("p t j -> p j t"))
         for js in pieces:
             nc.vector.quantize_mx(
                 out=xc_codes[:, js].bitcast(FP8X4), scales=xc_scale[:, js],
@@ -149,10 +150,11 @@ def tile_picked_codepage_plain_one_grouptriple_store_plain_kernel(
         for h, js in enumerate(pieces):
             bank = psum.tile([P, js.stop - js.start], F32, name=f"a0_bank{h}")
             first_product(bank[:], 0, js)
-            nc.scalar.activation(a[0][:, js], bank[:], COPY)
+            if h == 0:
+                nc.vector.tensor_copy(a[0][:, js], bank[:])
+            else:
+                nc.scalar.activation(a[0][:, js], bank[:], COPY)
 
-        vs_codes = sbuf.tile([P, N], U32, name="vs_codes", tag="xc_woven", align_bytes=64)
-        nc.vector.tensor_copy(vs_codes[:], vs_raw[:].bitcast(U32).indirect(l7[:]))
         for t in range(1, PACK):
             bank = psum.tile([P, J], F32, name=f"a_bank{t}")
             first_product(bank[:], t, slice(0, J))
@@ -171,9 +173,11 @@ def tile_picked_codepage_plain_one_grouptriple_store_plain_kernel(
 
         sum01 = sbuf.tile([P, 2, O], F32, name="sum01")
         triple_sum(sum01[:, 0, :], 0, 0, O, "s0")
-        vs_scale = sbuf.tile([P, N], U8, name="vs_scale", tag="s0_part0", align_bytes=64)
-        nc.vector.tensor_copy(vs_scale[:], vs_scale_raw[:].indirect(l7[:]))
+        vs_codes = sbuf.tile([P, N], U32, name="vs_codes", tag="s0_part0", align_bytes=64)
+        nc.vector.tensor_copy(vs_codes[:], vs_raw[:].bitcast(U32).indirect(l7[:]))
         triple_sum(sum01[:, 1, :], 1, 0, O, "s1")
+        vs_scale = sbuf.tile([P, N], U8, name="vs_scale", tag="s1_part0", align_bytes=64)
+        nc.vector.tensor_copy(vs_scale[:], vs_scale_raw[:].indirect(l7[:]))
         nc.vector.tensor_scalar_max(hid_woven[:, :, 0:2], sum01[:].rearrange("p t o -> p o t"), 0.0)
 
         hid_codes = sbuf.tile([P, O], U32, name="hid_codes", align_bytes=64)

@@ -128,9 +128,8 @@ def tile_picked_codepage_plain_one_grouptriple_store_plain_kernel(
         for h in range(2):
             js = slice(h * JH, (h + 1) * JH)
             fetch(xc23[:, 1, js], page[3], l3, h * JH, JH, gb_t, 3)
+            nc.vector.tensor_copy(xc_woven[:, js, 2:4], xc23[:, :, js].rearrange("p t j -> p j t"))
         pieces = [slice(0, JH), slice(JH, JH + JH // 2), slice(JH + JH // 2, J)]
-        for js, weave in zip(pieces, (nc.vector.tensor_copy, nc.vector.tensor_copy, nc.scalar.copy)):
-            weave(xc_woven[:, js, 2:4], xc23[:, :, js].rearrange("p t j -> p j t"))
         for js in pieces:
             nc.vector.quantize_mx(
                 out=xc_codes[:, js].bitcast(FP8X4), scales=xc_scale[:, js],

from contextlib import ExitStack

import concourse.mybir as mybir

K, J, R, T, U, O, N, S = 512, 512, 512, 1024, 1024, 256, 256, 1024
FLOPS = 2 * K * R * J + 2 * R * N * O

F32 = mybir.dt.float32
BF16 = mybir.dt.bfloat16
I32 = mybir.dt.int32
U32 = mybir.dt.uint32
U16 = mybir.dt.uint16
U8 = mybir.dt.uint8
FP8X4 = mybir.dt.float8_e4m3fn_x4
FP4X4 = mybir.dt.float4_e2m1fn_x4
COPY = mybir.ActivationFunctionType.Copy
ADD = mybir.AluOpType.add

P = 128
PACK = 4
LANES = 16
JH = J // 2
OH = O // 2
PAGES = 3


def tile_picked_codepage_plain_one_grouptriple_store_plain_kernel(
    tc, ta, ga, gb, w_words, w_scales, sa, sb, sd, vs_words, vs_scales,
    offs, offs2, offs3, offs4, offs5, offs6, offs7, out,
):
    nc = tc.nc
    with ExitStack() as ctx:
        lists = ctx.enter_context(tc.tile_pool(name="lists", bufs=1))
        sbuf = ctx.enter_context(tc.tile_pool(name="sbuf", bufs=1))
        psum = ctx.enter_context(tc.psum_pool(name="psum", bufs=1))

        def load_list(src, name):
            tile = lists.tile(list(src.shape), U16, name=name)
            nc.sync.dma_start(tile[:], src)
            return tile

        def load_factor(queue, src, name):
            tile = sbuf.tile([P, PACK], F32, name=name)
            queue.dma_start(tile[:], src.rearrange("(p t) o -> p (t o)", t=PACK))
            return tile

        def load_scale_rows(tile, src):
            for q in range(4):
                nc.sync.dma_start(tile[32 * q : 32 * q + 4, :].bitcast(I32), src[0, 4 * q : 4 * q + 4, :].bitcast(I32))

        ta_rows = ta.rearrange("(p t) c -> p t c", t=PACK)

        def load_table(queue, t):
            tile = sbuf.tile([P, T], F32, name=f"table{t}")
            queue.dma_start(tile[:], ta_rows[:, t, :])
            return tile

        page = [sbuf.tile([P, U], F32, name=f"page{t}") for t in range(PAGES)]
        page.append(page[0])
        w_scale_raw = sbuf.tile([P, R], U8, name="w_scale_raw", align_bytes=64)
        vs_scale_raw = sbuf.tile([P, S], U8, name="vs_scale_raw", align_bytes=64)
        warm = sbuf.tile([P, 2], F32, name="warm")
        nc.vector.memset(warm[:, 0:1], 0.0)
        nc.vector.memset(page[0][:], 0.0)
        nc.vector.memset(w_scale_raw[:].bitcast(I32), 0)
        nc.vector.memset(vs_scale_raw[:].bitcast(I32), 0)
        for t in range(1, PAGES):
            nc.vector.memset(page[t][:], 0.0)

        table = [load_table(nc.scalar, 0)]
        l1 = load_list(offs, "l1")
        ga_t = load_factor(nc.sync, ga, "ga_t")
        l2 = load_list(offs2, "l2")
        table.append(load_table(nc.scalar, 1))
        nc.scalar.activation(warm[:, 1:2], warm[:, 0:1], COPY)
        l3 = load_list(offs3, "l3")
        gb_t = load_factor(nc.sync, gb, "gb_t")
        l7 = load_list(offs7, "l7")
        table.append(load_table(nc.sync, 2))
        table.append(load_table(nc.sync, 3))
        w_raw = sbuf.tile([P, 2 * R], U8, name="w_raw", align_bytes=64)
        nc.sync.dma_start(w_raw[:].bitcast(I32), w_words[0].bitcast(I32))
        load_scale_rows(w_scale_raw, w_scales)
        vs_raw = sbuf.tile([P, S], I32, name="vs_raw", align_bytes=64)
        nc.sync.dma_start(vs_raw[:], vs_words[0].rearrange("p n t -> p (n t)").bitcast(I32))
        l4 = load_list(offs4, "l4")
        l5 = load_list(offs5, "l5")
        l6 = load_list(offs6, "l6")
        sa_t = load_factor(nc.sync, sa, "sa_t")
        sb_t = load_factor(nc.sync, sb, "sb_t")
        sd_t = load_factor(nc.sync, sd, "sd_t")
        load_scale_rows(vs_scale_raw, vs_scales)

        def fetch(dst, window, offsets, first, count, factor, t):
            cols = slice(first // LANES, (first + count) // LANES)
            nc.scalar.activation(dst, window[:].indirect(offsets[:, cols]), COPY, scale=factor[:, t : t + 1])

        xcd = [sbuf.tile([P, J], F32, name=f"xcd{t}", align_bytes=64) for t in range(PACK)]
        for h in range(2):
            js = slice(h * JH, (h + 1) * JH)
            fetch(xcd[0][:, js], table[0], l1, h * JH, JH, ga_t, 0)
            nc.vector.tensor_copy(page[0][:].indirect(l2[:, h * JH // LANES : (h + 1) * JH // LANES]), xcd[0][:, js])
        for t in range(1, PACK):
            fetch(xcd[t][:], table[t], l1, 0, J, ga_t, t)
        for t in range(1, PAGES):
            nc.vector.tensor_copy(page[t][:].indirect(l2[:]), xcd[t][:])

        xc01 = sbuf.tile([P, 2, J], BF16, name="xc01", tag="table3")
        xc_woven = sbuf.tile([P, J, PACK], BF16, name="xc_woven", align_bytes=64)
        for t in range(2):
            fetch(xc01[:, t, :], page[t], l3, 0, J, gb_t, t)
        nc.vector.tensor_copy(page[3][:].indirect(l2[:]), xcd[3][:])
        nc.scalar.copy(xc_woven[:, :, 0:2], xc01[:].rearrange("p t j -> p j t"))
        w_dealt = sbuf.tile([P, 2 * R], U8, name="w_dealt", align_bytes=64)
        nc.scalar.copy(
            w_dealt[:].bitcast(U16).rearrange("p (t m) -> p t m", t=PACK),
            w_raw[:].bitcast(U16).rearrange("p (m t) -> p t m", t=PACK),
        )
        xc23 = sbuf.tile([P, 2, J], BF16, name="xc23", tag="table3")
        fetch(xc23[:, 0, :], page[2], l3, 0, J, gb_t, 2)
        w_scale = sbuf.tile([P, R], U8, name="w_scale", tag="xcd3", align_bytes=64)
        nc.vector.tensor_copy(
            w_scale[:].rearrange("p (t m) -> p t m", t=PACK),
            w_scale_raw[:].rearrange("p (m t) -> p t m", t=PACK),
        )
        xc_codes = sbuf.tile([P, J], U32, name="xc_codes", align_bytes=64)
        xc_scale = sbuf.tile([P, J], U8, name="xc_scale", align_bytes=64)
        for h in range(2):
            js = slice(h * JH, (h + 1) * JH)
            fetch(xc23[:, 1, js], page[3], l3, h * JH, JH, gb_t, 3)
            nc.vector.tensor_copy(xc_woven[:, js, 2:4], xc23[:, :, js].rearrange("p t j -> p j t"))
        pieces = [slice(0, JH), slice(JH, JH + JH // 2), slice(JH + JH // 2, J)]
        for js in pieces:
            nc.vector.quantize_mx(
                out=xc_codes[:, js].bitcast(FP8X4), scales=xc_scale[:, js],
                in_=xc_woven[:, js, :].rearrange("p j t -> p (j t)"),
            )

        def first_product(dst, t, js):
            nc.tensor.matmul_mx(
                out=dst,
                lhsT=w_dealt[:, 2 * P * t : 2 * P * (t + 1)].bitcast(FP4X4),
                lhsT_scale=w_scale[:, P * t : P * (t + 1)],
                rhs=xc_codes[:, js].bitcast(FP8X4), rhs_scale=xc_scale[:, js],
                start=True, stop=True,
            )

        a = [sbuf.tile([P, J], F32, name=f"a{t}") for t in range(PACK)]
        for h, js in enumerate(pieces):
            bank = psum.tile([P, js.stop - js.start], F32, name=f"a0_bank{h}")
            first_product(bank[:], 0, js)
            if h == 0:
                nc.vector.tensor_copy(a[0][:, js], bank[:])
            else:
                nc.scalar.activation(a[0][:, js], bank[:], COPY)

        for t in range(1, PACK):
            bank = psum.tile([P, J], F32, name=f"a_bank{t}")
            first_product(bank[:], t, slice(0, J))
            nc.vector.tensor_copy(a[t][:], bank[:])

        hid_woven = sbuf.tile([P, O, PACK], BF16, name="hid_woven", align_bytes=64)

        def triple_sum(dst, t, first, count, name):
            parts = [sbuf.tile([P, count], F32, name=f"{name}_part{i}", align_bytes=64) for i in range(3)]
            two = sbuf.tile([P, count], F32, name=f"{name}_two")
            fetch(parts[0][:], a[t], l4, first, count, sa_t, t)
            fetch(parts[1][:], a[t], l5, first, count, sb_t, t)
            nc.vector.tensor_tensor(two[:], parts[0][:], parts[1][:], ADD)
            fetch(parts[2][:], a[t], l6, first, count, sd_t, t)
            nc.vector.tensor_tensor(dst, two[:], parts[2][:], ADD)

        sum01 = sbuf.tile([P, 2, O], F32, name="sum01")
        triple_sum(sum01[:, 0, :], 0, 0, O, "s0")
        vs_codes = sbuf.tile([P, N], U32, name="vs_codes", tag="s0_part0", align_bytes=64)
        nc.vector.tensor_copy(vs_codes[:], vs_raw[:].bitcast(U32).indirect(l7[:]))
        triple_sum(sum01[:, 1, :], 1, 0, O, "s1")
        vs_scale = sbuf.tile([P, N], U8, name="vs_scale", tag="s1_part0", align_bytes=64)
        nc.vector.tensor_copy(vs_scale[:], vs_scale_raw[:].indirect(l7[:]))
        nc.vector.tensor_scalar_max(hid_woven[:, :, 0:2], sum01[:].rearrange("p t o -> p o t"), 0.0)

        hid_codes = sbuf.tile([P, O], U32, name="hid_codes", align_bytes=64)
        hid_scale = sbuf.tile([P, O], U8, name="hid_scale", align_bytes=64)
        out_rows = out.rearrange("(m p) o -> p m o", p=P)

        def second_product(dst, m, os_):
            nc.tensor.matmul_mx(
                out=dst,
                lhsT=vs_codes[:, P * m : P * (m + 1)].bitcast(FP8X4),
                lhsT_scale=vs_scale[:, P * m : P * (m + 1)],
                rhs=hid_codes[:, os_].bitcast(FP8X4), rhs_scale=hid_scale[:, os_],
                start=True, stop=True,
            )

        for h in range(2):
            os_ = slice(h * OH, (h + 1) * OH)
            sum23 = sbuf.tile([P, 2, OH], F32, name=f"sum23_{h}")
            for t in range(2, PACK):
                triple_sum(sum23[:, t - 2, :], t, h * OH, OH, f"s{t}{h}")
            nc.vector.tensor_scalar_max(hid_woven[:, os_, 2:4], sum23[:].rearrange("p t o -> p o t"), 0.0)
            nc.vector.quantize_mx(
                out=hid_codes[:, os_].bitcast(FP8X4), scales=hid_scale[:, os_],
                in_=hid_woven[:, os_, :].rearrange("p o t -> p (o t)"),
            )
            if h == 0:
                bank0 = psum.tile([P, 2, OH], F32, name="y_bank", tag="a0_bank0")
                for m in range(2):
                    second_product(bank0[:, m, :], m, os_)
            else:
                y0 = sbuf.tile([P, 2, OH], F32, name="y0")
                nc.scalar.activation(y0[:], bank0[:], COPY)
                nc.sync.dma_start(out_rows[:, :, 0:OH], y0[:])
                for m in range(2):
                    bank = psum.tile([P, OH], F32, name=f"y1_bank{m}")
                    y = sbuf.tile([P, OH], F32, name=f"y1{m}")
                    second_product(bank[:], m, os_)
                    if m == 0:
                        nc.vector.tensor_copy(y[:], bank[:])
                        nc.sync.dma_start(out_rows[:, m, os_], y[:])
                    else:
                        nc.scalar.activation(y[:], bank[:], COPY)
                        nc.scalar.dma_start(out_rows[:, m, os_], y[:])
